import numpy as np
import ml_dtypes


def mxq(x, axis, fmt="e4m3"):
    dtype, down = {"e4m3": (ml_dtypes.float8_e4m3fn, 7), "e5m2": (ml_dtypes.float8_e5m2, 14)}[fmt]
    v = np.moveaxis(np.asarray(x, np.float32).astype(ml_dtypes.bfloat16).astype(np.float64), axis, -1)
    blocks = v.reshape(v.shape[:-1] + (-1, 32))
    amax = np.abs(blocks).max(-1, keepdims=True)
    byte = np.maximum(np.where(amax > 0, np.frexp(amax)[1] - 1 + 127, 0) - down, 1)
    scale = np.exp2(byte - 127.0)
    codes = (blocks / scale).astype(np.float32).astype(dtype).astype(np.float64)
    return np.moveaxis((codes * scale).reshape(v.shape), -1, axis)


WIDE = False


def mx_kscale(k):
    if not WIDE:
        return np.ones(k)
    levels = np.array([10, -10, 5, -5, 0])
    if k % 512:
        return np.exp2(np.random.permutation(np.resize(levels, k // 32))).repeat(32)
    a = np.empty((k // 512, 16))
    for p in range(k // 512):
        a[p, :8] = np.random.permutation(np.resize(levels, 8))
        for g in range(8):
            far = levels[np.abs(levels - a[p, g]) >= 10]
            a[p, g + 8] = far[np.random.randint(len(far))]
    return np.exp2(a.ravel()).repeat(32)


def f64(x):
    return np.asarray(x).astype(np.float64)


def striped(idx):
    return np.tile(idx.reshape(-1, 16).T, (8, 1)).astype(np.uint16)


def unstriped(offs):
    return offs[:16].T.reshape(-1).astype(np.int64)


E2M1 = np.array([0.0, 0.5, 1.0, 1.5, 2.0, 3.0, 4.0, 6.0, -0.0, -0.5, -1.0, -1.5, -2.0, -3.0, -4.0, -6.0])


def pack_weight(w, fmt):
    k, n = w.shape
    w = f64(np.asarray(w, np.float32).astype(ml_dtypes.bfloat16)).reshape(k // 32, 32, n)
    amax = np.abs(w).max(1)
    if fmt == "e4m3":
        byte = np.frexp(amax)[1] - 1 + 127 - 7
    else:
        mant, ex = np.frexp(amax / 6.0)
        byte = np.where(mant > 0.5, ex, ex - 1) + 127
    byte = np.clip(np.where(amax > 0, byte, 1), 1, 254)
    scaled = (w * np.exp2(127.0 - byte)[:, None, :]).reshape(k, n).astype(np.float32)
    by_word = np.ascontiguousarray(scaled.reshape(k // 512, 128, 4, n).transpose(0, 1, 3, 2))
    if fmt == "e4m3":
        words = by_word.astype(ml_dtypes.float8_e4m3fn).view(np.uint8)
    else:
        c = by_word.astype(ml_dtypes.float4_e2m1fn).view(np.uint8) & 0xF
        words = (c[..., 0::2] | (c[..., 1::2] << 4)).reshape(k // 512, 128, 2 * n)
    return np.ascontiguousarray(words), np.ascontiguousarray(byte.astype(np.uint8).reshape(k // 512, 16, n))


def unpack_weight(words, scales, fmt):
    g, _, n = scales.shape
    words = np.ascontiguousarray(words).reshape(g, 128, n, -1)
    if fmt == "e4m3":
        vals = words.view(ml_dtypes.float8_e4m3fn).astype(np.float64)
    else:
        nib = np.empty((g, 128, n, 4), np.uint8)
        nib[..., 0::2] = words & 0xF
        nib[..., 1::2] = words >> 4
        vals = E2M1[nib]
    vals = vals * np.repeat(np.exp2(scales.astype(np.float64) - 127.0), 8, axis=1)[..., None]
    return vals.transpose(0, 1, 3, 2).reshape(g * 512, n)


def gelu(v):
    return 0.5 * v * (1.0 + np.tanh(np.sqrt(2.0 / np.pi) * (v + 0.044715 * v**3)))


K, T, S, H, N, T2, P = 1024, 4096, 1024, 512, 768, 2048, 1024

def setup_inputs():
    n = np.random.standard_normal
    s = mx_kscale(K)[:, None]
    u = mx_kscale(H)[:, None]
    d = {}
    d["tab_words"], d["tab_scales"] = pack_weight(n((K, T)) * s, "e4m3")
    d["offs"] = striped(np.random.permutation(T)[:S])
    d["w1"] = (0.57 * n((K, H)) / K ** 0.5 / s).astype(np.float32)
    d["w2_words"], d["w2_scales"] = pack_weight(1.2 * n((K, H)) / K ** 0.5 / s * u.T, "e2m1")
    d["w3"] = (n((K, H)) / K ** 0.5 / s * u.T).astype(np.float32)
    d["page0"] = (n((H, T2)) * u).astype(np.float32)
    d["wgs"] = np.exp(0.3 * n((128, S))).astype(np.float32)
    d["offs2"] = striped(np.random.permutation(T2)[:S])
    d["offs3"] = striped(np.random.permutation(T2)[:P])
    d["gain"] = np.exp(0.3 * n(H)).astype(np.float32)
    d["w4_words"], d["w4_scales"] = pack_weight(n((H, N)) / H ** 0.5 / u, "e4m3")
    d["page1"] = (0.3 * n((N, T2))).astype(np.float32)
    d["wgo"] = np.exp(0.3 * n((128, P))).astype(np.float32)
    d["offs4"] = striped(np.random.permutation(T2)[:P])
    return d

def reference(tab_words, tab_scales, offs, w1, w2_words, w2_scales, w3, page0, wgs, offs2,
              offs3, gain, w4_words, w4_scales, page1, wgo, offs4):
    v = unpack_weight(tab_words, tab_scales, "e4m3")[:, unstriped(offs)]
    w2 = unpack_weight(w2_words, w2_scales, "e2m1")
    w4 = unpack_weight(w4_words, w4_scales, "e4m3")
    ph = mxq(f64(w1), 0, "e4m3").T @ v
    b = w2.T @ v
    skip = mxq(f64(w3), 0, "e4m3").T @ v
    h = np.minimum(b * np.cos(ph), skip)
    page = f64(page0).copy()
    page[:, unstriped(offs2)] = np.tile(f64(wgs), (H // 128, 1)) * h
    x = f64(gain)[:, None] * page[:, unstriped(offs3)]
    y = w4.T @ mxq(x, 0, "e4m3")
    y = y * np.exp(-np.abs(y))
    out = f64(page1).copy()
    out[:, unstriped(offs4)] = np.tile(f64(wgo), (N // 128, 1)) * y
    return out

@@ -1,0 +1,463 @@
+import math
+from contextlib import ExitStack
+
+import concourse.mybir as mybir
+from concourse.masks import make_identity
+
+K, T, S, H, N, T2, M = 1024, 4096, 1024, 512, 768, 2048, 1024
+FLOPS = 2 * (3 * K * H * S + H * N * M)
+
+F32 = mybir.dt.float32
+BF16 = mybir.dt.bfloat16
+I32 = mybir.dt.int32
+U32 = mybir.dt.uint32
+U16 = mybir.dt.uint16
+U8 = mybir.dt.uint8
+FP8X4 = mybir.dt.float8_e4m3fn_x4
+FP4X4 = mybir.dt.float4_e2m1fn_x4
+ACT = mybir.ActivationFunctionType
+ALU = mybir.AluOpType
+
+P = 128
+PACK = 4
+PASSES = K // (P * PACK)
+BANK = 512
+HALVES = S // BANK
+ROUND = 12582912.0
+PIECES = ((0, 256), (256, 512), (768, 256))
+EARLY = 768
+OPT = {"g": "mod", "gfirst": 512, "warm_sin": 1, "warm_exp": 1, "pin_from": 1, "late_at": 4, "late_pin": 2}
+
+
+def tile_list_masker_page_refit_kernel(
+    tc, tab_words, tab_scales, offs, w1, w2_words, w2_scales, w3, page0, wgs, offs2,
+    offs3, gain, w4_words, w4_scales, page1, wgo, offs4, out,
+):
+    nc = tc.nc
+    with ExitStack() as ctx:
+        lists = ctx.enter_context(tc.tile_pool(name="lists", bufs=1))
+        keep = ctx.enter_context(tc.tile_pool(name="keep", bufs=1))
+        ring = ctx.enter_context(tc.tile_pool(name="ring", bufs=2))
+        psum = ctx.enter_context(tc.psum_pool(name="psum", bufs=1))
+
+        def load_list(name, source):
+            tile = lists.tile([P, source.shape[1]], U16, name=name)
+            nc.sync.dma_start(tile[:], source)
+            return tile
+
+        def kept(name, shape, dtype, tag=None):
+            return keep.tile(shape, dtype, name=name, tag=tag or name, align_bytes=64)
+
+        def entries(tile, first, count):
+            return tile[:, first // 16 : (first + count) // 16]
+
+        tab_planes = kept("tab_planes", [P, T], U8)
+        w2_planes_raw = kept("w2_planes_raw", [P, PASSES, H], U8)
+        v_plane1 = kept("v_plane1", [P, S], U8)
+        w4_plane = kept("w4_plane", [P, N], U8)
+        for plane in (tab_planes, w2_planes_raw, v_plane1, w4_plane):
+            nc.vector.memset(plane[:].bitcast(I32), 0)
+
+        ident = kept("ident", [P, P], F32)
+        make_identity(nc, ident[:])
+        minus_round = kept("minus_round", [P, P], F32)
+        nc.vector.memset(minus_round[:], -ROUND)
+
+        if OPT.get("warm_sin"):
+            warm = kept("warm", [P, 16], F32)
+            nc.scalar.activation(warm[:, 0:1], ident[:, 0:1], ACT.Sin)
+        def load_weight(name, w, a, tag):
+            raw = kept(name, [P, PACK, H], F32, tag=tag)
+            nc.sync.dma_start(raw[:], w[512 * a : 512 * (a + 1), :].rearrange("(p j) c -> p j c", j=PACK))
+            return raw
+
+        def load_table(a):
+            words = kept("tab%d" % a, [P, T], U32)
+            nc.sync.dma_start(words[:].bitcast(I32), tab_words[a].rearrange("p t i -> p (t i)").bitcast(I32))
+            return words
+
+        w1_raw = [load_weight("w1_raw0", w1, 0, "wide0")]
+        idx = load_list("idx", offs)
+        w2_raw = kept("w2_raw", [P, PASSES, 2 * H], U8)
+        nc.sync.dma_start(w2_raw[:].bitcast(I32), w2_words.rearrange("a p c -> p a c").bitcast(I32))
+        w1_raw.append(load_weight("w1_raw1", w1, 1, "wide1"))
+        idx2 = load_list("idx2", offs2)
+        gain_sb = kept("gain_sb", [P, PACK], F32)
+        nc.sync.dma_start(gain_sb[:], gain.rearrange("(p t) -> p t", t=PACK))
+        for q in range(4):
+            nc.sync.dma_start(
+                tab_planes[32 * q : 32 * q + 4 * PASSES, :].bitcast(I32),
+                tab_scales[:, 4 * q : 4 * q + 4, :].bitcast(I32),
+            )
+        tab = [load_table(0)]
+        for q in range(4):
+            nc.sync.dma_start(
+                w2_planes_raw[32 * q : 32 * q + 4, :, :].bitcast(I32),
+                w2_scales[:, 4 * q : 4 * q + 4, :].rearrange("a r c -> r a c").bitcast(I32),
+            )
+        tab.append(load_table(1))
+        w3_raw = [load_weight("w3_raw%d" % a, w3, a, "wide%d" % (PASSES + a)) for a in range(PASSES)]
+
+        page0_rows = page0.rearrange("(p t) n -> t p n", t=PACK)
+        wgs_rows = wgs.rearrange("(b t) j -> t b j", t=PACK)
+        state, state_weight = [], []
+
+        def load_state(t):
+            weight = kept("wgs%d" % t, [P, S], F32)
+            for a in range(4):
+                nc.sync.dma_start(weight[32 * a : 32 * (a + 1), :], wgs_rows[t])
+            rows = kept("state%d" % t, [P, T2], F32)
+            nc.sync.dma_start(rows[:], page0_rows[t])
+            state.append(rows)
+            state_weight.append(weight)
+
+        load_state(0)
+        idx3 = load_list("idx3", offs3)
+        load_state(1)
+        wgo_sb = kept("wgo_sb", [P, M], F32)
+        nc.sync.dma_start(wgo_sb[:], wgo)
+        load_state(2)
+        load_state(3)
+        idx4 = load_list("idx4", offs4)
+        w4_codes = kept("w4_codes", [P, N], U32)
+        nc.sync.dma_start(w4_codes[:].bitcast(I32), w4_words[0].rearrange("p c i -> p (c i)").bitcast(I32))
+        for q in range(4):
+            nc.sync.dma_start(
+                w4_plane[32 * q : 32 * q + 4, :].bitcast(I32),
+                w4_scales[0, 4 * q : 4 * q + 4, :].bitcast(I32),
+            )
+
+        v_plane0 = kept("v_plane0", [P, S], U8)
+        nc.vector.tensor_copy(v_plane0[:], tab_planes[:].indirect(idx[:]))
+        nc.scalar.dma_start(v_plane1[0:112, :].bitcast(I32), v_plane0[4:116, :].bitcast(I32))
+        v_planes = (v_plane0[:], v_plane1[:])
+        packed_planes = (v_plane0[:], v_plane0[4:P, :])
+
+        w2_codes = kept("w2_codes", [P, PASSES * 2 * H], U8)
+        nc.vector.tensor_copy(
+            w2_codes[:].rearrange("p (a t m e) -> p a t m e", a=PASSES, t=PACK, e=2),
+            w2_raw[:].rearrange("p a (m t e) -> p a t m e", t=PACK, e=2),
+        )
+
+        def quantise_weight(name, raw, cast, grouped):
+            cast(
+                grouped.rearrange("p (t m j) -> p m j t", t=PACK, j=PACK),
+                raw[:].rearrange("p j (m t) -> p m j t", t=PACK),
+            )
+            codes = kept(name + "_codes", [P, H], U32)
+            plane = kept(name + "_plane", [P, H], U8)
+            nc.vector.quantize_mx(codes[:].bitcast(FP8X4), plane[:], grouped)
+            return codes, plane
+
+        w1_q = []
+        for a in range(PASSES):
+            grouped = kept("w1_bf16_%d" % a, [P, PACK * H], BF16, tag="half%d" % a)
+            w1_q.append(quantise_weight("w1_%d" % a, w1_raw[a], nc.scalar.copy, grouped[:]))
+
+        w2_planes = kept("w2_planes", [P, PASSES * H], U8, tag="half1")
+        nc.vector.tensor_copy(
+            w2_planes[:].rearrange("p (a t m) -> p a t m", a=PASSES, t=PACK),
+            w2_planes_raw[:].rearrange("p a (m t) -> p a t m", t=PACK),
+        )
+
+        v_codes = []
+        for a, tag in enumerate(("tab_planes", "tab0")):
+            picked = kept("v%d" % a, [P, S], U32, tag=tag)
+            halves = [picked[:, BANK * half : BANK * (half + 1)] for half in range(HALVES)]
+            for half in range(HALVES):
+                nc.vector.tensor_copy(halves[half], tab[a][:].indirect(entries(idx, BANK * half, BANK)))
+            v_codes.append(picked)
+
+        w3_bf16 = kept("w3_bf16", [P, PASSES * PACK * H], BF16, tag="tab1")
+        w3_q = [
+            quantise_weight(
+                "w3_%d" % a, w3_raw[a], nc.vector.tensor_copy, w3_bf16[:, PACK * H * a : PACK * H * (a + 1)]
+            )
+            for a in range(PASSES)
+        ]
+
+        masker = []
+        for c in range(N // P):
+            rows = kept("masker%d" % c, [P, T2], F32, tag="wide%d" % c)
+            nc.sync.dma_start(rows[:], page1[P * c : P * (c + 1), :])
+            masker.append(rows)
+
+        def block(i):
+            return slice(P * i, P * (i + 1))
+
+        def add_transposed(target, terms):
+            for n, term in enumerate(terms):
+                nc.tensor.matmul(
+                    target, term, ident[:], start=(n == 0), stop=(n == len(terms) - 1), is_transpose=True
+                )
+
+        def bank(name, kind, n, depth):
+            return psum.tile([P, BANK], F32, name=name, tag="%s%d" % (kind, n % depth))
+
+        def cosine(step, t, first, count):
+            phase = bank("phase", "turned", step, 2)
+            for i in range(count // P):
+                for a in range(PASSES):
+                    codes, plane = w1_q[a]
+                    nc.tensor.matmul_mx(
+                        out=phase[:, block(i)],
+                        lhsT=v_codes[a][:, block(first // P + i)].bitcast(FP8X4),
+                        lhsT_scale=packed_planes[a][:, block(first // P + i)],
+                        rhs=codes[:, block(t)].bitcast(FP8X4),
+                        rhs_scale=plane[:, block(t)],
+                        start=(a == 0),
+                        stop=(a == PASSES - 1),
+                    )
+            turns = kept("turns", [P, count], F32, tag="turns%d" % (step % 2))
+            nc.scalar.activation(turns[:], phase[:, 0:count], ACT.Copy, bias=0.25, scale=1.0 / (2.0 * math.pi))
+            whole = kept("whole", [P, count], F32, tag="whole%d" % (step % 2))
+            nc.scalar.activation(whole[:], turns[:], ACT.Copy, bias=ROUND, scale=-1.0)
+            fraction = bank("fraction", "sum", step, 4)
+            for i in range(count // P):
+                add_transposed(fraction[:, block(i)], (whole[:, block(i)], minus_round[:], turns[:, block(i)]))
+            cos = kept("cos", [P, count], F32, tag="cos%d" % (step % 2))
+            nc.scalar.activation(cos[:], fraction[:, 0:count], ACT.Sin, scale=2.0 * math.pi)
+            return cos
+
+        def modulate(step, t, first, count):
+            cos = cosine(step, t, first, count)
+            cols = slice(first, first + count)
+            b = bank("b", "plain", step, 2)
+            for a in range(PASSES):
+                slot = PACK * a + t
+                for n0 in range(0, count, 512 if count == 512 else 128):
+                  w = 512 if count == 512 else 128
+                  nc.tensor.matmul_mx(
+                    out=b[:, n0:n0 + w],
+                    lhsT=w2_codes[:, 2 * P * slot : 2 * P * (slot + 1)].bitcast(FP4X4),
+                    lhsT_scale=w2_planes[:, block(slot)],
+                    rhs=v_codes[a][:, first + n0:first + n0 + w].bitcast(FP8X4),
+                    rhs_scale=v_planes[a][:, first + n0:first + n0 + w],
+                    start=(a == 0),
+                    stop=(a == PASSES - 1),
+                  )
+            if OPT.get("g") == "mod" and t > 0 and first == OPT.get("gfirst", 0):
+                modulated = kept("modulated", [P, BANK], F32, tag="recall%d" % (t - 1))
+            else:
+                modulated = ring.tile([P, BANK], F32, name="modulated", tag="fourth")
+            nc.vector.tensor_tensor(modulated[:, 0:count], b[:, 0:count], cos[:], ALU.mult)
+            return modulated[:, 0:count]
+
+        def bound(step, t, first, count):
+            cols = slice(first, first + count)
+            lag = 1 if step >= OPT.get("pin_from", 0) else 2
+            skip = bank("skip", "sum", step + lag, 4)
+            for a in range(PASSES):
+                codes, plane = w3_q[a]
+                nc.tensor.matmul_mx(
+                    out=skip[:, 0:count],
+                    lhsT=codes[:, block(t)].bitcast(FP8X4),
+                    lhsT_scale=plane[:, block(t)],
+                    rhs=v_codes[a][:, cols].bitcast(FP8X4),
+                    rhs_scale=packed_planes[a][:, cols],
+                    start=(a == 0),
+                    stop=(a == PASSES - 1),
+                )
+            return skip[:, 0:count]
+
+        recalled_early = []
+
+        def recall_early(t):
+            recalled = kept("recalled", [P, EARLY], F32, tag="recall%d" % t)
+            nc.vector.tensor_copy(recalled[:], state[t][:].indirect(entries(idx3, 0, EARLY)))
+            recalled_early.append(recalled)
+
+        hs = {}
+        def put_states(step, t, first, count, modulated):
+            skip = bound(step, t, first, count)
+            if OPT.get("wide") and t >= OPT["wide"]:
+                if first == 0:
+                    hs[t] = kept("h", [P, S], F32, tag="hw%d" % (t % 2))
+                nc.vector.tensor_tensor(hs[t][:, first:first + count], skip, modulated, ALU.min)
+                if first + count == S:
+                    recall_early(t - 1)
+                    nc.vector.tensor_tensor(state[t][:].indirect(idx2[:]), hs[t][:], state_weight[t][:], ALU.mult)
+                return
+            h = ring.tile([P, BANK], F32, name="h", tag="fifth")
+            nc.vector.tensor_tensor(h[:, 0:count], skip, modulated, ALU.min)
+            if first == OPT.get("gfirst", 0) and t > 0:
+                recall_early(t - 1)
+            nc.vector.tensor_tensor(
+                state[t][:].indirect(entries(idx2, first, count)),
+                h[:, 0:count],
+                state_weight[t][:, first : first + count],
+                ALU.mult,
+            )
+
+        steps = [(t, BANK * half, BANK) for t in range(PACK) for half in range(HALVES)]
+        if OPT.get("split"):
+            steps = [(0, 0, 256), (0, 256, 256)] + steps[1:]
+        ready = modulate(0, *steps[0])
+        for n, step in enumerate(steps):
+            current = ready
+            if n == 0 and OPT.get("pin_from", 0) > 0:
+                put_states(n, *step, current)
+            if n + 1 < len(steps):
+                ready = modulate(n + 1, *steps[n + 1])
+            if not (n == 0 and OPT.get("pin_from", 0) > 0):
+                put_states(n, *step, current)
+        last = (len(steps) - 1) % 2
+
+        minus_log_wgo = kept("minus_log_wgo", [P, M], F32)
+
+        def turn_log_wgo():
+            log_wgo = kept("log_wgo", [P, M], F32, tag="cos%d" % last)
+            nc.scalar.activation(log_wgo[:], wgo_sb[:], ACT.Ln)
+            for half in range(M // BANK):
+                turned = bank("log_turned", "turned", half, 2)
+                for i in range(BANK // P):
+                    nc.tensor.transpose(turned[:, block(i)], log_wgo[:, block(4 * half + i)], ident[:])
+                nc.scalar.activation(minus_log_wgo[:, BANK * half : BANK * (half + 1)], turned[:], ACT.Copy, scale=-1.0)
+
+            if OPT.get("warm_exp"):
+                warm2 = kept("warm2", [P, 16], F32)
+                nc.scalar.activation(warm2[:, 0:1], minus_log_wgo[:, M - 1 : M], ACT.Exp)
+
+        def weave(x, t, source):
+            nc.scalar.activation(x[:, :, t], source, ACT.Copy, scale=gain_sb[:, t : t + 1])
+
+        def quantise_x(name, x):
+            count = x.shape[1]
+            codes = kept(name + "_codes", [P, count], U32)
+            plane = kept(name + "_plane", [P, count], U8)
+            nc.vector.quantize_mx(codes[:].bitcast(FP8X4), plane[:], x[:].rearrange("p m t -> p (m t)"))
+            return codes, plane
+
+        early = PIECES[:-1]
+        x_early = [
+            kept("x%d" % n, [P, count, PACK], BF16, tag=tag)
+            for (n, (first, count)), tag in zip(enumerate(early), ("whole%d" % last, "turns%d" % last))
+        ]
+        for t in range(PACK - 1):
+            if t == PACK - 2:
+                turn_log_wgo()
+            for x, (first, count) in zip(x_early, early):
+                weave(x, t, recalled_early[t][:, first : first + count])
+        x_q = []
+        for n, (first, count) in enumerate(early):
+            last_rows = kept("last_rows%d" % n, [P, count], F32)
+            nc.vector.tensor_copy(last_rows[:], state[PACK - 1][:].indirect(entries(idx3, first, count)))
+            weave(x_early[n], PACK - 1, last_rows[:])
+        x_q.append(quantise_x("x0", x_early[0]))
+
+        late_first, late_count = PIECES[-1]
+        recalled_late = kept("recalled_late", [P, PACK, late_count], F32, tag="whole%d" % last)
+        for t in range(PACK):
+            nc.vector.tensor_copy(
+                recalled_late[:, t, :], state[t][:].indirect(entries(idx3, late_first, late_count))
+            )
+        x_q.append(quantise_x("x1", x_early[1]))
+
+        def prepare_late_x():
+            x = kept("x_late", [P, late_count, PACK], BF16, tag="opening")
+            for t in range(PACK):
+                weave(x, t, recalled_late[:, t, :])
+            x_q.append(quantise_x("x_late", x))
+
+        def put_scores(n, first_tile, left, right):
+            first, count = PIECES[n]
+            for c in range(BANK // count):
+                tile = first_tile + c
+                nc.vector.tensor_tensor(
+                    masker[tile][:].indirect(entries(idx4, first, count)), left(c), right(c), ALU.mult
+                )
+                missing[tile].remove(n)
+                if not missing[tile]:
+                    nc.sync.dma_start(out[P * tile : P * (tile + 1), :], masker[tile][:])
+
+        def opening_scores():
+            first, count = PIECES[0]
+            codes, plane = x_q[0]
+            y = bank("y_opening", "plain", 0, 2)
+            for c in range(BANK // count):
+                nc.tensor.matmul_mx(
+                    out=y[:, count * c : count * (c + 1)],
+                    lhsT=w4_codes[:, block(c)].bitcast(FP8X4),
+                    lhsT_scale=w4_plane[:, block(c)],
+                    rhs=codes[:].bitcast(FP8X4),
+                    rhs_scale=plane[:],
+                    start=True,
+                    stop=True,
+                )
+            size = kept("size_opening", [P, BANK], F32, tag="turns%d" % (1 - last))
+            nc.scalar.activation(size[:], y[:], ACT.Abs)
+            fade = kept("fade", [P, BANK], F32, tag="whole%d" % (1 - last))
+            nc.scalar.activation(fade[:], size[:], ACT.Exp, scale=-1.0)
+            faded = ring.tile([P, BANK], F32, name="faded", tag="fifth")
+            nc.vector.tensor_tensor(faded[:], y[:], fade[:], ALU.mult)
+            return faded
+
+        def turn_scores(job, n, first_tile):
+            first, count = PIECES[n]
+            blocks = count // P
+            tiles = BANK // count
+            codes, plane = x_q[n]
+            turned = bank("y_turned", "turned", job, 2)
+            cols = slice(P * first_tile, P * (first_tile + tiles))
+            for i in range(blocks):
+                nc.tensor.matmul_mx(
+                    out=turned[:, P * tiles * i : P * tiles * (i + 1)],
+                    lhsT=codes[:, block(i)].bitcast(FP8X4),
+                    lhsT_scale=plane[:, block(i)],
+                    rhs=w4_codes[:, cols].bitcast(FP8X4),
+                    rhs_scale=w4_plane[:, cols],
+                    start=True,
+                    stop=True,
+                )
+            if job == OPT.get("late_pin", 2):
+                size = kept("size", [P, BANK], F32, tag="opening")
+            else:
+                size = ring.tile([P, BANK], F32, name="size", tag="first")
+            nc.scalar.activation(size[:], turned[:], ACT.Abs)
+            value = ring.tile([P, BANK], F32, name="value", tag="second")
+            nc.scalar.copy(value[:], turned[:])
+            exponent = bank("exponent", "sum", job, 4)
+            y = bank("y", "plain", job, 2)
+            for c in range(tiles):
+                for i in range(blocks):
+                    add_transposed(
+                        exponent[:, block(blocks * c + i)],
+                        (size[:, block(tiles * i + c)], minus_log_wgo[:, block(first // P + i)]),
+                    )
+            for c in range(tiles):
+                for i in range(blocks):
+                    nc.tensor.transpose(y[:, block(blocks * c + i)], value[:, block(tiles * i + c)], ident[:])
+            return exponent, y
+
+        def finish_scores(n, first_tile, exponent, y):
+            count = PIECES[n][1]
+            factor = ring.tile([P, BANK], F32, name="factor", tag="factor", bufs=3)
+            nc.scalar.activation(factor[:], exponent[:], ACT.Exp, scale=-1.0)
+            y_sb = ring.tile([P, BANK], F32, name="y_sb", tag="y_sb", bufs=3)
+            nc.scalar.copy(y_sb[:], y[:])
+            put_scores(
+                n,
+                first_tile,
+                lambda c: y_sb[:, count * c : count * (c + 1)],
+                lambda c: factor[:, count * c : count * (c + 1)],
+            )
+
+        tiles = N // P
+        missing = [list(range(len(PIECES))) for tile in range(tiles)]
+        jobs = (
+            [(0, c) for c in range(0, tiles, 2)]
+            + [(1, c) for c in range(tiles // 2)]
+            + [(2, c) for c in range(0, tiles, 2)]
+            + [(1, c) for c in range(tiles // 2, tiles)]
+        )
+        faded = opening_scores()
+        ready = turn_scores(1, *jobs[1])
+        count = PIECES[0][1]
+        put_scores(*jobs[0], lambda c: faded[:, count * c : count * (c + 1)], lambda c: wgo_sb[:, 0:count])
+        for j in range(1, len(jobs)):
+            current = ready
+            if j + 1 < len(jobs):
+                if j + 1 == OPT.get("late_at", 6):
+                    prepare_late_x()
+                ready = turn_scores(j + 1, *jobs[j + 1])
+            finish_scores(*jobs[j], *current)

@@ -26,7 +26,7 @@ HALVES = S // BANK
 ROUND = 12582912.0
 PIECES = ((0, 256), (256, 512), (768, 256))
 EARLY = 768
-OPT = {"g": "mod", "gfirst": 512, "warm_sin": 1, "warm_exp": 1, "pin_from": 1, "late_at": 4, "late_pin": 2}
+OPT = {"g": "mod", "gfirst": 512, "warm_sin": 1, "warm_exp": 1, "pin_from": 1, "late_at": 4, "late_pin": 2, "ln_step": 6, "twice": (2, 4, 6, 8, 10)}
 
 
 def tile_list_masker_page_refit_kernel(
@@ -55,7 +55,7 @@ def tile_list_masker_page_refit_kernel(
         w2_planes_raw = kept("w2_planes_raw", [P, PASSES, H], U8)
         v_plane1 = kept("v_plane1", [P, S], U8)
         w4_plane = kept("w4_plane", [P, N], U8)
-        for plane in (tab_planes, w2_planes_raw, v_plane1, w4_plane):
+        for plane in ((w2_planes_raw, tab_planes, v_plane1, w4_plane) if OPT.get("pool_ts") else (tab_planes, w2_planes_raw, v_plane1, w4_plane)):
             nc.vector.memset(plane[:].bitcast(I32), 0)
 
         ident = kept("ident", [P, P], F32)
@@ -85,16 +85,20 @@ def tile_list_masker_page_refit_kernel(
         gain_sb = kept("gain_sb", [P, PACK], F32)
         nc.sync.dma_start(gain_sb[:], gain.rearrange("(p t) -> p t", t=PACK))
         for q in range(4):
-            nc.sync.dma_start(
+            (nc.gpsimd if OPT.get("pool_ts") else nc.sync).dma_start(
                 tab_planes[32 * q : 32 * q + 4 * PASSES, :].bitcast(I32),
                 tab_scales[:, 4 * q : 4 * q + 4, :].bitcast(I32),
             )
-        tab = [load_table(0)]
+        tab = []
+        if not OPT.get("pool_ts"):
+            tab.append(load_table(0))
         for q in range(4):
             nc.sync.dma_start(
                 w2_planes_raw[32 * q : 32 * q + 4, :, :].bitcast(I32),
                 w2_scales[:, 4 * q : 4 * q + 4, :].rearrange("a r c -> r a c").bitcast(I32),
             )
+        if OPT.get("pool_ts"):
+            tab.append(load_table(0))
         tab.append(load_table(1))
         w3_raw = [load_weight("w3_raw%d" % a, w3, a, "wide%d" % (PASSES + a)) for a in range(PASSES)]
 
@@ -104,10 +108,14 @@ def tile_list_masker_page_refit_kernel(
 
         def load_state(t):
             weight = kept("wgs%d" % t, [P, S], F32)
+            cut = BANK if (t == 0 and OPT.get("wcut")) else S
             for a in range(4):
-                nc.sync.dma_start(weight[32 * a : 32 * (a + 1), :], wgs_rows[t])
+                nc.sync.dma_start(weight[32 * a : 32 * (a + 1), 0:cut], wgs_rows[t][:, 0:cut])
             rows = kept("state%d" % t, [P, T2], F32)
             nc.sync.dma_start(rows[:], page0_rows[t])
+            if cut < S:
+                for a in range(4):
+                    nc.sync.dma_start(weight[32 * a : 32 * (a + 1), cut:S], wgs_rows[t][:, cut:S])
             state.append(rows)
             state_weight.append(weight)
 
@@ -129,7 +137,7 @@ def tile_list_masker_page_refit_kernel(
 
         v_plane0 = kept("v_plane0", [P, S], U8)
         nc.vector.tensor_copy(v_plane0[:], tab_planes[:].indirect(idx[:]))
-        nc.scalar.dma_start(v_plane1[0:112, :].bitcast(I32), v_plane0[4:116, :].bitcast(I32))
+        (nc.gpsimd if OPT.get("pool_shift") else nc.scalar).dma_start(v_plane1[0:112, :].bitcast(I32), v_plane0[4:116, :].bitcast(I32))
         v_planes = (v_plane0[:], v_plane1[:])
         packed_planes = (v_plane0[:], v_plane0[4:P, :])
 
@@ -144,7 +152,7 @@ def tile_list_masker_page_refit_kernel(
                 grouped.rearrange("p (t m j) -> p m j t", t=PACK, j=PACK),
                 raw[:].rearrange("p j (m t) -> p m j t", t=PACK),
             )
-            codes = kept(name + "_codes", [P, H], U32)
+            codes = kept(name + "_codes", [P, H], U32, tag="tab_planes" if (name == "w1_1" and OPT.get("qpin")) else None)
             plane = kept(name + "_plane", [P, H], U8)
             nc.vector.quantize_mx(codes[:].bitcast(FP8X4), plane[:], grouped)
             return codes, plane
@@ -161,7 +169,7 @@ def tile_list_masker_page_refit_kernel(
         )
 
         v_codes = []
-        for a, tag in enumerate(("tab_planes", "tab0")):
+        for a, tag in enumerate(("half1" if OPT.get("qpin") else "tab_planes", "tab0")):
             picked = kept("v%d" % a, [P, S], U32, tag=tag)
             halves = [picked[:, BANK * half : BANK * (half + 1)] for half in range(HALVES)]
             for half in range(HALVES):
@@ -213,10 +221,19 @@ def tile_list_masker_page_refit_kernel(
             whole = kept("whole", [P, count], F32, tag="whole%d" % (step % 2))
             nc.scalar.activation(whole[:], turns[:], ACT.Copy, bias=ROUND, scale=-1.0)
             fraction = bank("fraction", "sum", step, 4)
-            for i in range(count // P):
+            if step >= OPT.get("four", 99):
+                less = kept("less", [P, count], F32, tag="less%d" % (step % 2))
+                nc.scalar.activation(less[:], whole[:], ACT.Copy, bias=-ROUND)
+                for i in range(count // P):
+                    add_transposed(fraction[:, block(i)], (less[:, block(i)], turns[:, block(i)]))
+            else:
+              for i in range(count // P):
                 add_transposed(fraction[:, block(i)], (whole[:, block(i)], minus_round[:], turns[:, block(i)]))
-            cos = kept("cos", [P, count], F32, tag="cos%d" % (step % 2))
+            cos = kept("cos", [P, count], F32, tag="lnpin" if step == OPT["ln_step"] else "cos%d" % (step % 2))
             nc.scalar.activation(cos[:], fraction[:, 0:count], ACT.Sin, scale=2.0 * math.pi)
+            if OPT.get("warm_exp") and step == len(steps) - 1:
+                warm2 = kept("warm2", [P, 16], F32)
+                nc.scalar.activation(warm2[:, 0:1], cos[:, 0:1], ACT.Exp)
             return cos
 
         def modulate(step, t, first, count):
@@ -289,6 +306,18 @@ def tile_list_masker_page_refit_kernel(
                 ALU.mult,
             )
 
+        minus_log_wgo = kept("minus_log_wgo", [P, M], F32)
+
+        def turn_log_wgo():
+            log_wgo = kept("log_wgo", [P, M], F32, tag="lnpin")
+            nc.scalar.activation(log_wgo[:], wgo_sb[:], ACT.Ln)
+            for half in range(M // BANK):
+                turned = bank("log_turned", OPT.get("lnbank", "turned"), half, 2)
+                for i in range(BANK // P):
+                    nc.tensor.transpose(turned[:, block(i)], log_wgo[:, block(4 * half + i)], ident[:])
+                nc.scalar.activation(minus_log_wgo[:, BANK * half : BANK * (half + 1)], turned[:], ACT.Copy, scale=-1.0)
+
+
         steps = [(t, BANK * half, BANK) for t in range(PACK) for half in range(HALVES)]
         if OPT.get("split"):
             steps = [(0, 0, 256), (0, 256, 256)] + steps[1:]
@@ -301,22 +330,9 @@ def tile_list_masker_page_refit_kernel(
                 ready = modulate(n + 1, *steps[n + 1])
             if not (n == 0 and OPT.get("pin_from", 0) > 0):
                 put_states(n, *step, current)
+            if n == OPT["ln_step"] + OPT.get("ln_text", 0):
+                turn_log_wgo()
         last = (len(steps) - 1) % 2
-
-        minus_log_wgo = kept("minus_log_wgo", [P, M], F32)
-
-        def turn_log_wgo():
-            log_wgo = kept("log_wgo", [P, M], F32, tag="cos%d" % last)
-            nc.scalar.activation(log_wgo[:], wgo_sb[:], ACT.Ln)
-            for half in range(M // BANK):
-                turned = bank("log_turned", "turned", half, 2)
-                for i in range(BANK // P):
-                    nc.tensor.transpose(turned[:, block(i)], log_wgo[:, block(4 * half + i)], ident[:])
-                nc.scalar.activation(minus_log_wgo[:, BANK * half : BANK * (half + 1)], turned[:], ACT.Copy, scale=-1.0)
-
-            if OPT.get("warm_exp"):
-                warm2 = kept("warm2", [P, 16], F32)
-                nc.scalar.activation(warm2[:, 0:1], minus_log_wgo[:, M - 1 : M], ACT.Exp)
 
         def weave(x, t, source):
             nc.scalar.activation(x[:, :, t], source, ACT.Copy, scale=gain_sb[:, t : t + 1])
@@ -331,11 +347,9 @@ def tile_list_masker_page_refit_kernel(
         early = PIECES[:-1]
         x_early = [
             kept("x%d" % n, [P, count, PACK], BF16, tag=tag)
-            for (n, (first, count)), tag in zip(enumerate(early), ("whole%d" % last, "turns%d" % last))
+            for (n, (first, count)), tag in zip(enumerate(early), (("less%d" if "four" in OPT else "whole%d") % last, "turns%d" % last))
         ]
         for t in range(PACK - 1):
-            if t == PACK - 2:
-                turn_log_wgo()
             for x, (first, count) in zip(x_early, early):
                 weave(x, t, recalled_early[t][:, first : first + count])
         x_q = []
@@ -346,7 +360,7 @@ def tile_list_masker_page_refit_kernel(
         x_q.append(quantise_x("x0", x_early[0]))
 
         late_first, late_count = PIECES[-1]
-        recalled_late = kept("recalled_late", [P, PACK, late_count], F32, tag="whole%d" % last)
+        recalled_late = kept("recalled_late", [P, PACK, late_count], F32, tag=("less%d" if "four" in OPT else "whole%d") % last)
         for t in range(PACK):
             nc.vector.tensor_copy(
                 recalled_late[:, t, :], state[t][:].indirect(entries(idx3, late_first, late_count))
@@ -370,27 +384,34 @@ def tile_list_masker_page_refit_kernel(
                 if not missing[tile]:
                     nc.sync.dma_start(out[P * tile : P * (tile + 1), :], masker[tile][:])
 
-        def opening_scores():
-            first, count = PIECES[0]
-            codes, plane = x_q[0]
-            y = bank("y_opening", "plain", 0, 2)
+        def plain_scores(y, n, first_tile):
+            first, count = PIECES[n]
+            codes, plane = x_q[n]
             for c in range(BANK // count):
                 nc.tensor.matmul_mx(
                     out=y[:, count * c : count * (c + 1)],
-                    lhsT=w4_codes[:, block(c)].bitcast(FP8X4),
-                    lhsT_scale=w4_plane[:, block(c)],
+                    lhsT=w4_codes[:, block(first_tile + c)].bitcast(FP8X4),
+                    lhsT_scale=w4_plane[:, block(first_tile + c)],
                     rhs=codes[:].bitcast(FP8X4),
                     rhs_scale=plane[:],
                     start=True,
                     stop=True,
                 )
-            size = kept("size_opening", [P, BANK], F32, tag="turns%d" % (1 - last))
+
+        def short_scores(job, n, first_tile):
+            y = bank("y_short", "plain", job, 2)
+            plain_scores(y, n, first_tile)
+            size = ring.tile([P, BANK], F32, name="size", tag="first")
             nc.scalar.activation(size[:], y[:], ACT.Abs)
-            fade = kept("fade", [P, BANK], F32, tag="whole%d" % (1 - last))
+            fade = ring.tile([P, BANK], F32, name="fade", tag="second")
             nc.scalar.activation(fade[:], size[:], ACT.Exp, scale=-1.0)
+            return y, fade
+
+        def finish_short(job, n, first_tile, y, fade):
+            first, count = PIECES[n]
             faded = ring.tile([P, BANK], F32, name="faded", tag="fifth")
             nc.vector.tensor_tensor(faded[:], y[:], fade[:], ALU.mult)
-            return faded
+            put_scores(n, first_tile, lambda c: faded[:, count * c : count * (c + 1)], lambda c: wgo_sb[:, first : first + count])
 
         def turn_scores(job, n, first_tile):
             first, count = PIECES[n]
@@ -414,17 +435,21 @@ def tile_list_masker_page_refit_kernel(
             else:
                 size = ring.tile([P, BANK], F32, name="size", tag="first")
             nc.scalar.activation(size[:], turned[:], ACT.Abs)
-            value = ring.tile([P, BANK], F32, name="value", tag="second")
-            nc.scalar.copy(value[:], turned[:])
+            twice = job in OPT.get("twice", ())
+            if not twice:
+                value = ring.tile([P, BANK], F32, name="value", tag="second")
+                nc.scalar.copy(value[:], turned[:])
             exponent = bank("exponent", "sum", job, 4)
             y = bank("y", "plain", job, 2)
+            if twice:
+                plain_scores(y, n, first_tile)
             for c in range(tiles):
                 for i in range(blocks):
                     add_transposed(
                         exponent[:, block(blocks * c + i)],
                         (size[:, block(tiles * i + c)], minus_log_wgo[:, block(first // P + i)]),
                     )
-            for c in range(tiles):
+            for c in range(0 if twice else tiles):
                 for i in range(blocks):
                     nc.tensor.transpose(y[:, block(blocks * c + i)], value[:, block(tiles * i + c)], ident[:])
             return exponent, y
@@ -450,14 +475,15 @@ def tile_list_masker_page_refit_kernel(
             + [(2, c) for c in range(0, tiles, 2)]
             + [(1, c) for c in range(tiles // 2, tiles)]
         )
-        faded = opening_scores()
-        ready = turn_scores(1, *jobs[1])
-        count = PIECES[0][1]
-        put_scores(*jobs[0], lambda c: faded[:, count * c : count * (c + 1)], lambda c: wgo_sb[:, 0:count])
-        for j in range(1, len(jobs)):
+        short = OPT.get("short", (0,))
+        ready = short_scores(0, *jobs[0])
+        for j in range(len(jobs)):
             current = ready
             if j + 1 < len(jobs):
                 if j + 1 == OPT.get("late_at", 6):
                     prepare_late_x()
-                ready = turn_scores(j + 1, *jobs[j + 1])
-            finish_scores(*jobs[j], *current)
+                ready = (short_scores if j + 1 in short else turn_scores)(j + 1, *jobs[j + 1])
+            if j in short:
+                finish_short(j, *jobs[j], *current)
+            else:
+                finish_scores(*jobs[j], *current)

import math
from contextlib import ExitStack

import concourse.mybir as mybir
from concourse.masks import make_identity

K, T, S, H, N, T2, M = 1024, 4096, 1024, 512, 768, 2048, 1024
FLOPS = 2 * (3 * K * H * S + H * N * M)

F32 = mybir.dt.float32
BF16 = mybir.dt.bfloat16
I32 = mybir.dt.int32
U32 = mybir.dt.uint32
U16 = mybir.dt.uint16
U8 = mybir.dt.uint8
FP8X4 = mybir.dt.float8_e4m3fn_x4
FP4X4 = mybir.dt.float4_e2m1fn_x4
ACT = mybir.ActivationFunctionType
ALU = mybir.AluOpType

P = 128
PACK = 4
PASSES = K // (P * PACK)
BANK = 512
HALVES = S // BANK
ROUND = 12582912.0
PIECES = ((0, 256), (256, 512), (768, 256))
EARLY = 768
OPT = {"g": "mod", "gfirst": 512, "warm_sin": 1, "warm_exp": 1, "pin_from": 1, "late_at": 4, "late_pin": 2, "ln_step": 6, "twice": (2, 4, 6, 8, 10)}


def tile_list_masker_page_refit_kernel(
    tc, tab_words, tab_scales, offs, w1, w2_words, w2_scales, w3, page0, wgs, offs2,
    offs3, gain, w4_words, w4_scales, page1, wgo, offs4, out,
):
    nc = tc.nc
    with ExitStack() as ctx:
        lists = ctx.enter_context(tc.tile_pool(name="lists", bufs=1))
        keep = ctx.enter_context(tc.tile_pool(name="keep", bufs=1))
        ring = ctx.enter_context(tc.tile_pool(name="ring", bufs=2))
        psum = ctx.enter_context(tc.psum_pool(name="psum", bufs=1))

        def load_list(name, source):
            tile = lists.tile([P, source.shape[1]], U16, name=name)
            nc.sync.dma_start(tile[:], source)
            return tile

        def kept(name, shape, dtype, tag=None):
            return keep.tile(shape, dtype, name=name, tag=tag or name, align_bytes=64)

        def entries(tile, first, count):
            return tile[:, first // 16 : (first + count) // 16]

        tab_planes = kept("tab_planes", [P, T], U8)
        w2_planes_raw = kept("w2_planes_raw", [P, PASSES, H], U8)
        v_plane1 = kept("v_plane1", [P, S], U8)
        w4_plane = kept("w4_plane", [P, N], U8)
        for plane in ((w2_planes_raw, tab_planes, v_plane1, w4_plane) if OPT.get("pool_ts") else (tab_planes, w2_planes_raw, v_plane1, w4_plane)):
            nc.vector.memset(plane[:].bitcast(I32), 0)

        ident = kept("ident", [P, P], F32)
        make_identity(nc, ident[:])
        minus_round = kept("minus_round", [P, P], F32)
        nc.vector.memset(minus_round[:], -ROUND)

        if OPT.get("warm_sin"):
            warm = kept("warm", [P, 16], F32)
            nc.scalar.activation(warm[:, 0:1], ident[:, 0:1], ACT.Sin)
        def load_weight(name, w, a, tag):
            raw = kept(name, [P, PACK, H], F32, tag=tag)
            nc.sync.dma_start(raw[:], w[512 * a : 512 * (a + 1), :].rearrange("(p j) c -> p j c", j=PACK))
            return raw

        def load_table(a):
            words = kept("tab%d" % a, [P, T], U32)
            nc.sync.dma_start(words[:].bitcast(I32), tab_words[a].rearrange("p t i -> p (t i)").bitcast(I32))
            return words

        w1_raw = [load_weight("w1_raw0", w1, 0, "wide0")]
        idx = load_list("idx", offs)
        w2_raw = kept("w2_raw", [P, PASSES, 2 * H], U8)
        nc.sync.dma_start(w2_raw[:].bitcast(I32), w2_words.rearrange("a p c -> p a c").bitcast(I32))
        w1_raw.append(load_weight("w1_raw1", w1, 1, "wide1"))
        idx2 = load_list("idx2", offs2)
        gain_sb = kept("gain_sb", [P, PACK], F32)
        nc.sync.dma_start(gain_sb[:], gain.rearrange("(p t) -> p t", t=PACK))
        for q in range(4):
            (nc.gpsimd if OPT.get("pool_ts") else nc.sync).dma_start(
                tab_planes[32 * q : 32 * q + 4 * PASSES, :].bitcast(I32),
                tab_scales[:, 4 * q : 4 * q + 4, :].bitcast(I32),
            )
        tab = []
        if not OPT.get("pool_ts"):
            tab.append(load_table(0))
        for q in range(4):
            nc.sync.dma_start(
                w2_planes_raw[32 * q : 32 * q + 4, :, :].bitcast(I32),
                w2_scales[:, 4 * q : 4 * q + 4, :].rearrange("a r c -> r a c").bitcast(I32),
            )
        if OPT.get("pool_ts"):
            tab.append(load_table(0))
        tab.append(load_table(1))
        w3_raw = [load_weight("w3_raw%d" % a, w3, a, "wide%d" % (PASSES + a)) for a in range(PASSES)]

        page0_rows = page0.rearrange("(p t) n -> t p n", t=PACK)
        wgs_rows = wgs.rearrange("(b t) j -> t b j", t=PACK)
        state, state_weight = [], []

        def load_state(t):
            weight = kept("wgs%d" % t, [P, S], F32)
            cut = BANK if (t == 0 and OPT.get("wcut")) else S
            for a in range(4):
                nc.sync.dma_start(weight[32 * a : 32 * (a + 1), 0:cut], wgs_rows[t][:, 0:cut])
            rows = kept("state%d" % t, [P, T2], F32)
            nc.sync.dma_start(rows[:], page0_rows[t])
            if cut < S:
                for a in range(4):
                    nc.sync.dma_start(weight[32 * a : 32 * (a + 1), cut:S], wgs_rows[t][:, cut:S])
            state.append(rows)
            state_weight.append(weight)

        load_state(0)
        idx3 = load_list("idx3", offs3)
        load_state(1)
        wgo_sb = kept("wgo_sb", [P, M], F32)
        nc.sync.dma_start(wgo_sb[:], wgo)
        load_state(2)
        load_state(3)
        idx4 = load_list("idx4", offs4)
        w4_codes = kept("w4_codes", [P, N], U32)
        nc.sync.dma_start(w4_codes[:].bitcast(I32), w4_words[0].rearrange("p c i -> p (c i)").bitcast(I32))
        for q in range(4):
            nc.sync.dma_start(
                w4_plane[32 * q : 32 * q + 4, :].bitcast(I32),
                w4_scales[0, 4 * q : 4 * q + 4, :].bitcast(I32),
            )

        v_plane0 = kept("v_plane0", [P, S], U8)
        nc.vector.tensor_copy(v_plane0[:], tab_planes[:].indirect(idx[:]))
        (nc.gpsimd if OPT.get("pool_shift") else nc.scalar).dma_start(v_plane1[0:112, :].bitcast(I32), v_plane0[4:116, :].bitcast(I32))
        v_planes = (v_plane0[:], v_plane1[:])
        packed_planes = (v_plane0[:], v_plane0[4:P, :])

        w2_codes = kept("w2_codes", [P, PASSES * 2 * H], U8)
        nc.vector.tensor_copy(
            w2_codes[:].rearrange("p (a t m e) -> p a t m e", a=PASSES, t=PACK, e=2),
            w2_raw[:].rearrange("p a (m t e) -> p a t m e", t=PACK, e=2),
        )

        def quantise_weight(name, raw, cast, grouped):
            cast(
                grouped.rearrange("p (t m j) -> p m j t", t=PACK, j=PACK),
                raw[:].rearrange("p j (m t) -> p m j t", t=PACK),
            )
            codes = kept(name + "_codes", [P, H], U32, tag="tab_planes" if (name == "w1_1" and OPT.get("qpin")) else None)
            plane = kept(name + "_plane", [P, H], U8)
            nc.vector.quantize_mx(codes[:].bitcast(FP8X4), plane[:], grouped)
            return codes, plane

        w1_q = []
        for a in range(PASSES):
            grouped = kept("w1_bf16_%d" % a, [P, PACK * H], BF16, tag="half%d" % a)
            w1_q.append(quantise_weight("w1_%d" % a, w1_raw[a], nc.scalar.copy, grouped[:]))

        w2_planes = kept("w2_planes", [P, PASSES * H], U8, tag="half1")
        nc.vector.tensor_copy(
            w2_planes[:].rearrange("p (a t m) -> p a t m", a=PASSES, t=PACK),
            w2_planes_raw[:].rearrange("p a (m t) -> p a t m", t=PACK),
        )

        v_codes = []
        for a, tag in enumerate(("half1" if OPT.get("qpin") else "tab_planes", "tab0")):
            picked = kept("v%d" % a, [P, S], U32, tag=tag)
            halves = [picked[:, BANK * half : BANK * (half + 1)] for half in range(HALVES)]
            for half in range(HALVES):
                nc.vector.tensor_copy(halves[half], tab[a][:].indirect(entries(idx, BANK * half, BANK)))
            v_codes.append(picked)

        w3_bf16 = kept("w3_bf16", [P, PASSES * PACK * H], BF16, tag="tab1")
        w3_q = [
            quantise_weight(
                "w3_%d" % a, w3_raw[a], nc.vector.tensor_copy, w3_bf16[:, PACK * H * a : PACK * H * (a + 1)]
            )
            for a in range(PASSES)
        ]

        masker = []
        for c in range(N // P):
            rows = kept("masker%d" % c, [P, T2], F32, tag="wide%d" % c)
            nc.sync.dma_start(rows[:], page1[P * c : P * (c + 1), :])
            masker.append(rows)

        def block(i):
            return slice(P * i, P * (i + 1))

        def add_transposed(target, terms):
            for n, term in enumerate(terms):
                nc.tensor.matmul(
                    target, term, ident[:], start=(n == 0), stop=(n == len(terms) - 1), is_transpose=True
                )

        def bank(name, kind, n, depth):
            return psum.tile([P, BANK], F32, name=name, tag="%s%d" % (kind, n % depth))

        def cosine(step, t, first, count):
            phase = bank("phase", "turned", step, 2)
            for i in range(count // P):
                for a in range(PASSES):
                    codes, plane = w1_q[a]
                    nc.tensor.matmul_mx(
                        out=phase[:, block(i)],
                        lhsT=v_codes[a][:, block(first // P + i)].bitcast(FP8X4),
                        lhsT_scale=packed_planes[a][:, block(first // P + i)],
                        rhs=codes[:, block(t)].bitcast(FP8X4),
                        rhs_scale=plane[:, block(t)],
                        start=(a == 0),
                        stop=(a == PASSES - 1),
                    )
            turns = kept("turns", [P, count], F32, tag="turns%d" % (step % 2))
            nc.scalar.activation(turns[:], phase[:, 0:count], ACT.Copy, bias=0.25, scale=1.0 / (2.0 * math.pi))
            whole = kept("whole", [P, count], F32, tag="whole%d" % (step % 2))
            nc.scalar.activation(whole[:], turns[:], ACT.Copy, bias=ROUND, scale=-1.0)
            fraction = bank("fraction", "sum", step, 4)
            if step >= OPT.get("four", 99):
                less = kept("less", [P, count], F32, tag="less%d" % (step % 2))
                nc.scalar.activation(less[:], whole[:], ACT.Copy, bias=-ROUND)
                for i in range(count // P):
                    add_transposed(fraction[:, block(i)], (less[:, block(i)], turns[:, block(i)]))
            else:
              for i in range(count // P):
                add_transposed(fraction[:, block(i)], (whole[:, block(i)], minus_round[:], turns[:, block(i)]))
            cos = kept("cos", [P, count], F32, tag="lnpin" if step == OPT["ln_step"] else "cos%d" % (step % 2))
            nc.scalar.activation(cos[:], fraction[:, 0:count], ACT.Sin, scale=2.0 * math.pi)
            if OPT.get("warm_exp") and step == len(steps) - 1:
                warm2 = kept("warm2", [P, 16], F32)
                nc.scalar.activation(warm2[:, 0:1], cos[:, 0:1], ACT.Exp)
            return cos

        def modulate(step, t, first, count):
            cos = cosine(step, t, first, count)
            cols = slice(first, first + count)
            b = bank("b", "plain", step, 2)
            for a in range(PASSES):
                slot = PACK * a + t
                for n0 in range(0, count, 512 if count == 512 else 128):
                  w = 512 if count == 512 else 128
                  nc.tensor.matmul_mx(
                    out=b[:, n0:n0 + w],
                    lhsT=w2_codes[:, 2 * P * slot : 2 * P * (slot + 1)].bitcast(FP4X4),
                    lhsT_scale=w2_planes[:, block(slot)],
                    rhs=v_codes[a][:, first + n0:first + n0 + w].bitcast(FP8X4),
                    rhs_scale=v_planes[a][:, first + n0:first + n0 + w],
                    start=(a == 0),
                    stop=(a == PASSES - 1),
                  )
            if OPT.get("g") == "mod" and t > 0 and first == OPT.get("gfirst", 0):
                modulated = kept("modulated", [P, BANK], F32, tag="recall%d" % (t - 1))
            else:
                modulated = ring.tile([P, BANK], F32, name="modulated", tag="fourth")
            nc.vector.tensor_tensor(modulated[:, 0:count], b[:, 0:count], cos[:], ALU.mult)
            return modulated[:, 0:count]

        def bound(step, t, first, count):
            cols = slice(first, first + count)
            lag = 1 if step >= OPT.get("pin_from", 0) else 2
            skip = bank("skip", "sum", step + lag, 4)
            for a in range(PASSES):
                codes, plane = w3_q[a]
                nc.tensor.matmul_mx(
                    out=skip[:, 0:count],
                    lhsT=codes[:, block(t)].bitcast(FP8X4),
                    lhsT_scale=plane[:, block(t)],
                    rhs=v_codes[a][:, cols].bitcast(FP8X4),
                    rhs_scale=packed_planes[a][:, cols],
                    start=(a == 0),
                    stop=(a == PASSES - 1),
                )
            return skip[:, 0:count]

        recalled_early = []

        def recall_early(t):
            recalled = kept("recalled", [P, EARLY], F32, tag="recall%d" % t)
            nc.vector.tensor_copy(recalled[:], state[t][:].indirect(entries(idx3, 0, EARLY)))
            recalled_early.append(recalled)

        hs = {}
        def put_states(step, t, first, count, modulated):
            skip = bound(step, t, first, count)
            if OPT.get("wide") and t >= OPT["wide"]:
                if first == 0:
                    hs[t] = kept("h", [P, S], F32, tag="hw%d" % (t % 2))
                nc.vector.tensor_tensor(hs[t][:, first:first + count], skip, modulated, ALU.min)
                if first + count == S:
                    recall_early(t - 1)
                    nc.vector.tensor_tensor(state[t][:].indirect(idx2[:]), hs[t][:], state_weight[t][:], ALU.mult)
                return
            h = ring.tile([P, BANK], F32, name="h", tag="fifth")
            nc.vector.tensor_tensor(h[:, 0:count], skip, modulated, ALU.min)
            if first == OPT.get("gfirst", 0) and t > 0:
                recall_early(t - 1)
            nc.vector.tensor_tensor(
                state[t][:].indirect(entries(idx2, first, count)),
                h[:, 0:count],
                state_weight[t][:, first : first + count],
                ALU.mult,
            )

        minus_log_wgo = kept("minus_log_wgo", [P, M], F32)

        def turn_log_wgo():
            log_wgo = kept("log_wgo", [P, M], F32, tag="lnpin")
            nc.scalar.activation(log_wgo[:], wgo_sb[:], ACT.Ln)
            for half in range(M // BANK):
                turned = bank("log_turned", OPT.get("lnbank", "turned"), half, 2)
                for i in range(BANK // P):
                    nc.tensor.transpose(turned[:, block(i)], log_wgo[:, block(4 * half + i)], ident[:])
                nc.scalar.activation(minus_log_wgo[:, BANK * half : BANK * (half + 1)], turned[:], ACT.Copy, scale=-1.0)


        steps = [(t, BANK * half, BANK) for t in range(PACK) for half in range(HALVES)]
        if OPT.get("split"):
            steps = [(0, 0, 256), (0, 256, 256)] + steps[1:]
        ready = modulate(0, *steps[0])
        for n, step in enumerate(steps):
            current = ready
            if n == 0 and OPT.get("pin_from", 0) > 0:
                put_states(n, *step, current)
            if n + 1 < len(steps):
                ready = modulate(n + 1, *steps[n + 1])
            if not (n == 0 and OPT.get("pin_from", 0) > 0):
                put_states(n, *step, current)
            if n == OPT["ln_step"] + OPT.get("ln_text", 0):
                turn_log_wgo()
        last = (len(steps) - 1) % 2

        def weave(x, t, source):
            nc.scalar.activation(x[:, :, t], source, ACT.Copy, scale=gain_sb[:, t : t + 1])

        def quantise_x(name, x):
            count = x.shape[1]
            codes = kept(name + "_codes", [P, count], U32)
            plane = kept(name + "_plane", [P, count], U8)
            nc.vector.quantize_mx(codes[:].bitcast(FP8X4), plane[:], x[:].rearrange("p m t -> p (m t)"))
            return codes, plane

        early = PIECES[:-1]
        x_early = [
            kept("x%d" % n, [P, count, PACK], BF16, tag=tag)
            for (n, (first, count)), tag in zip(enumerate(early), (("less%d" if "four" in OPT else "whole%d") % last, "turns%d" % last))
        ]
        for t in range(PACK - 1):
            for x, (first, count) in zip(x_early, early):
                weave(x, t, recalled_early[t][:, first : first + count])
        x_q = []
        for n, (first, count) in enumerate(early):
            last_rows = kept("last_rows%d" % n, [P, count], F32)
            nc.vector.tensor_copy(last_rows[:], state[PACK - 1][:].indirect(entries(idx3, first, count)))
            weave(x_early[n], PACK - 1, last_rows[:])
        x_q.append(quantise_x("x0", x_early[0]))

        late_first, late_count = PIECES[-1]
        recalled_late = kept("recalled_late", [P, PACK, late_count], F32, tag=("less%d" if "four" in OPT else "whole%d") % last)
        for t in range(PACK):
            nc.vector.tensor_copy(
                recalled_late[:, t, :], state[t][:].indirect(entries(idx3, late_first, late_count))
            )
        x_q.append(quantise_x("x1", x_early[1]))

        def prepare_late_x():
            x = kept("x_late", [P, late_count, PACK], BF16, tag="opening")
            for t in range(PACK):
                weave(x, t, recalled_late[:, t, :])
            x_q.append(quantise_x("x_late", x))

        def put_scores(n, first_tile, left, right):
            first, count = PIECES[n]
            for c in range(BANK // count):
                tile = first_tile + c
                nc.vector.tensor_tensor(
                    masker[tile][:].indirect(entries(idx4, first, count)), left(c), right(c), ALU.mult
                )
                missing[tile].remove(n)
                if not missing[tile]:
                    nc.sync.dma_start(out[P * tile : P * (tile + 1), :], masker[tile][:])

        def plain_scores(y, n, first_tile):
            first, count = PIECES[n]
            codes, plane = x_q[n]
            for c in range(BANK // count):
                nc.tensor.matmul_mx(
                    out=y[:, count * c : count * (c + 1)],
                    lhsT=w4_codes[:, block(first_tile + c)].bitcast(FP8X4),
                    lhsT_scale=w4_plane[:, block(first_tile + c)],
                    rhs=codes[:].bitcast(FP8X4),
                    rhs_scale=plane[:],
                    start=True,
                    stop=True,
                )

        def short_scores(job, n, first_tile):
            y = bank("y_short", "plain", job, 2)
            plain_scores(y, n, first_tile)
            size = ring.tile([P, BANK], F32, name="size", tag="first")
            nc.scalar.activation(size[:], y[:], ACT.Abs)
            fade = ring.tile([P, BANK], F32, name="fade", tag="second")
            nc.scalar.activation(fade[:], size[:], ACT.Exp, scale=-1.0)
            return y, fade

        def finish_short(job, n, first_tile, y, fade):
            first, count = PIECES[n]
            faded = ring.tile([P, BANK], F32, name="faded", tag="fifth")
            nc.vector.tensor_tensor(faded[:], y[:], fade[:], ALU.mult)
            put_scores(n, first_tile, lambda c: faded[:, count * c : count * (c + 1)], lambda c: wgo_sb[:, first : first + count])

        def turn_scores(job, n, first_tile):
            first, count = PIECES[n]
            blocks = count // P
            tiles = BANK // count
            codes, plane = x_q[n]
            turned = bank("y_turned", "turned", job, 2)
            cols = slice(P * first_tile, P * (first_tile + tiles))
            for i in range(blocks):
                nc.tensor.matmul_mx(
                    out=turned[:, P * tiles * i : P * tiles * (i + 1)],
                    lhsT=codes[:, block(i)].bitcast(FP8X4),
                    lhsT_scale=plane[:, block(i)],
                    rhs=w4_codes[:, cols].bitcast(FP8X4),
                    rhs_scale=w4_plane[:, cols],
                    start=True,
                    stop=True,
                )
            if job == OPT.get("late_pin", 2):
                size = kept("size", [P, BANK], F32, tag="opening")
            else:
                size = ring.tile([P, BANK], F32, name="size", tag="first")
            nc.scalar.activation(size[:], turned[:], ACT.Abs)
            twice = job in OPT.get("twice", ())
            if not twice:
                value = ring.tile([P, BANK], F32, name="value", tag="second")
                nc.scalar.copy(value[:], turned[:])
            exponent = bank("exponent", "sum", job, 4)
            y = bank("y", "plain", job, 2)
            if twice:
                plain_scores(y, n, first_tile)
            for c in range(tiles):
                for i in range(blocks):
                    add_transposed(
                        exponent[:, block(blocks * c + i)],
                        (size[:, block(tiles * i + c)], minus_log_wgo[:, block(first // P + i)]),
                    )
            for c in range(0 if twice else tiles):
                for i in range(blocks):
                    nc.tensor.transpose(y[:, block(blocks * c + i)], value[:, block(tiles * i + c)], ident[:])
            return exponent, y

        def finish_scores(n, first_tile, exponent, y):
            count = PIECES[n][1]
            factor = ring.tile([P, BANK], F32, name="factor", tag="factor", bufs=3)
            nc.scalar.activation(factor[:], exponent[:], ACT.Exp, scale=-1.0)
            y_sb = ring.tile([P, BANK], F32, name="y_sb", tag="y_sb", bufs=3)
            nc.scalar.copy(y_sb[:], y[:])
            put_scores(
                n,
                first_tile,
                lambda c: y_sb[:, count * c : count * (c + 1)],
                lambda c: factor[:, count * c : count * (c + 1)],
            )

        tiles = N // P
        missing = [list(range(len(PIECES))) for tile in range(tiles)]
        jobs = (
            [(0, c) for c in range(0, tiles, 2)]
            + [(1, c) for c in range(tiles // 2)]
            + [(2, c) for c in range(0, tiles, 2)]
            + [(1, c) for c in range(tiles // 2, tiles)]
        )
        short = OPT.get("short", (0,))
        ready = short_scores(0, *jobs[0])
        for j in range(len(jobs)):
            current = ready
            if j + 1 < len(jobs):
                if j + 1 == OPT.get("late_at", 6):
                    prepare_late_x()
                ready = (short_scores if j + 1 in short else turn_scores)(j + 1, *jobs[j + 1])
            if j in short:
                finish_short(j, *jobs[j], *current)
            else:
                finish_scores(*jobs[j], *current)
